import numpy as np
import ml_dtypes


def mxq(x, axis, fmt="e4m3"):
    dtype, down = {"e4m3": (ml_dtypes.float8_e4m3fn, 7), "e5m2": (ml_dtypes.float8_e5m2, 14)}[fmt]
    v = np.moveaxis(np.asarray(x, np.float32).astype(ml_dtypes.bfloat16).astype(np.float64), axis, -1)
    blocks = v.reshape(v.shape[:-1] + (-1, 32))
    amax = np.abs(blocks).max(-1, keepdims=True)
    byte = np.maximum(np.where(amax > 0, np.frexp(amax)[1] - 1 + 127, 0) - down, 1)
    scale = np.exp2(byte - 127.0)
    codes = (blocks / scale).astype(np.float32).astype(dtype).astype(np.float64)
    return np.moveaxis((codes * scale).reshape(v.shape), -1, axis)


WIDE = False


def mx_kscale(k):
    if not WIDE:
        return np.ones(k)
    levels = np.array([10, -10, 5, -5, 0])
    if k % 512:
        return np.exp2(np.random.permutation(np.resize(levels, k // 32))).repeat(32)
    a = np.empty((k // 512, 16))
    for p in range(k // 512):
        a[p, :8] = np.random.permutation(np.resize(levels, 8))
        for g in range(8):
            far = levels[np.abs(levels - a[p, g]) >= 10]
            a[p, g + 8] = far[np.random.randint(len(far))]
    return np.exp2(a.ravel()).repeat(32)


def f64(x):
    return np.asarray(x).astype(np.float64)


def striped(idx):
    return np.tile(idx.reshape(-1, 16).T, (8, 1)).astype(np.uint16)


def unstriped(offs):
    return offs[:16].T.reshape(-1).astype(np.int64)


E2M1 = np.array([0.0, 0.5, 1.0, 1.5, 2.0, 3.0, 4.0, 6.0, -0.0, -0.5, -1.0, -1.5, -2.0, -3.0, -4.0, -6.0])


def pack_fp4(w):
    k, n = w.shape
    w = f64(np.asarray(w, np.float32).astype(ml_dtypes.bfloat16)).reshape(k // 32, 32, n)
    amax = np.abs(w).max(1)
    mant, ex = np.frexp(amax / 6.0)
    byte = np.clip(np.where(amax > 0, np.where(mant > 0.5, ex, ex - 1) + 127, 1), 1, 254)
    scaled = (w * np.exp2(127.0 - byte)[:, None, :]).reshape(k, n).astype(np.float32)
    c = np.ascontiguousarray(scaled.reshape(k // 512, 128, 4, n).transpose(0, 1, 3, 2)).astype(ml_dtypes.float4_e2m1fn).view(np.uint8) & 0xF
    words = (c[..., 0::2] | (c[..., 1::2] << 4)).reshape(k // 512, 128, 2 * n)
    return np.ascontiguousarray(words), np.ascontiguousarray(byte.astype(np.uint8).reshape(k // 512, 16, n))


def unpack_fp4(words, scales):
    g, _, n = scales.shape
    words = np.ascontiguousarray(words).reshape(g, 128, n, 2)
    nib = np.empty((g, 128, n, 4), np.uint8)
    nib[..., 0::2] = words & 0xF
    nib[..., 1::2] = words >> 4
    vals = E2M1[nib] * np.repeat(np.exp2(scales.astype(np.float64) - 127.0), 8, axis=1)[..., None]
    return vals.transpose(0, 1, 3, 2).reshape(g * 512, n)


def gelu(v):
    return 0.5 * v * (1.0 + np.tanh(np.sqrt(2.0 / np.pi) * (v + 0.044715 * v**3)))


K, T, S, V, N = 512, 4096, 1024, 512, 128
P = 2 ** 7


def setup_inputs():
    n = np.random.standard_normal
    s = mx_kscale(K)[:, None]
    packed_w1 = pack_fp4(n((K, N)) / np.sqrt(K) / s)
    return {
        "xT": (n((K, T)) * s).astype(np.float32),
        "w1_words": packed_w1[0],
        "w1_scales": packed_w1[1],
        "frac": np.tile(np.random.uniform(0.05, 0.95, V), (P, 1)).astype(np.float32),
        "offs": striped(np.random.permutation(T)[:S]),
        "left": striped(np.random.permutation(S)[:V]),
        "right": striped(np.random.permutation(S)[:V]),
    }


def reference(xT, w1_words, w1_scales, frac, offs, left, right):
    xq = mxq(f64(xT)[:, unstriped(offs)], 0, "e4m3")
    y = gelu(unpack_fp4(w1_words, w1_scales).T @ xq)
    l = y[:, unstriped(left)]
    return l + (y[:, unstriped(right)] - l) * f64(frac)[:1]

@@ -1,0 +1,125 @@
+from contextlib import ExitStack
+
+import concourse.mybir as mybir
+
+K, T, S, V, N = 512, 4096, 1024, 512, 128
+FLOPS = 2 * K * S * N
+
+F32 = mybir.dt.float32
+BF16 = mybir.dt.bfloat16
+I32 = mybir.dt.int32
+U32 = mybir.dt.uint32
+U16 = mybir.dt.uint16
+U8 = mybir.dt.uint8
+FP8X4 = mybir.dt.float8_e4m3fn_x4
+FP4X4 = mybir.dt.float4_e2m1fn_x4
+ACT = mybir.ActivationFunctionType
+ALU = mybir.AluOpType
+
+P = 128
+PACK = 4
+HALF = S // 2
+PIECE = 256
+LAST_CHUNKS = (1024, 1024, 1024, 768, 256)
+VECTOR_CHUNK = 3
+
+
+def tile_picked_lerp_gelu_e_kernel(tc, xT, w1_words, w1_scales, frac, offs, left, right, out):
+    nc = tc.nc
+    with ExitStack() as ctx:
+        keep = ctx.enter_context(tc.tile_pool(name="keep", bufs=1))
+        psum = ctx.enter_context(tc.psum_pool(name="psum", bufs=1))
+
+        offs_t = keep.tile([P, S // 16], U16, name="offs_t")
+        left_t = keep.tile([P, V // 16], U16, name="left_t")
+        right_t = keep.tile([P, V // 16], U16, name="right_t")
+        planes = [keep.tile([P, T], F32, name="plane%d" % t) for t in range(PACK)]
+        last_bf = keep.tile([P, T], BF16, name="last_bf")
+        grouped = keep.tile([P, S, PACK], BF16, name="grouped", align_bytes=64)
+        w_words = keep.tile([P, 2 * N], U8, name="w_words", align_bytes=64)
+        w_scales = keep.tile([P, N], U8, name="w_scales", align_bytes=64)
+        frac_t = keep.tile([P, V], F32, name="frac_t")
+        rest_t = keep.tile([P, V], F32, name="rest_t")
+        y = keep.tile([P, S], F32, name="y")
+        warm_in = keep.tile([P, 8], F32, name="warm_in")
+        warm_out = keep.tile([P, 8], F32, name="warm_out")
+
+        nc.gpsimd.memset(warm_in[:], 0.0)
+        nc.scalar.activation(warm_out[:], warm_in[:], ACT.Gelu_apprx_tanh)
+        nc.vector.memset(w_scales[:].bitcast(I32), 0)
+
+        rows = xT.rearrange("(p j) c -> p j c", j=PACK)
+        nc.sync.dma_start(planes[0][:], rows[:, 0, :])
+        nc.sync.dma_start(offs_t[:], offs)
+        nc.sync.dma_start(planes[1][:], rows[:, 1, :])
+        nc.sync.dma_start(planes[2][:], rows[:, 2, :])
+        spans = []
+        c0 = 0
+        for width in LAST_CHUNKS:
+            spans.append(slice(c0, c0 + width))
+            c0 = c0 + width
+        for cols in spans:
+            nc.sync.dma_start(planes[3][:, cols], rows[:, 3, cols])
+        nc.sync.dma_start(w_words[:].bitcast(I32), w1_words[0].bitcast(I32))
+        for q in range(4):
+            nc.sync.dma_start(
+                w_scales[32 * q : 32 * q + 4, :].bitcast(I32),
+                w1_scales[0, 4 * q : 4 * q + 4, :].bitcast(I32),
+            )
+        nc.sync.dma_start(frac_t[:], frac)
+        nc.sync.dma_start(left_t[:], left)
+        nc.sync.dma_start(right_t[:], right)
+
+        for t in range(PACK - 1):
+            nc.vector.tensor_copy(grouped[:, :, t], planes[t][:].indirect(offs_t[:]))
+        for i, cols in enumerate(spans):
+            if i == VECTOR_CHUNK:
+                nc.vector.tensor_copy(last_bf[:, cols], planes[3][:, cols])
+            else:
+                nc.scalar.activation(last_bf[:, cols], planes[3][:, cols], ACT.Copy)
+        nc.vector.tensor_copy(grouped[:, :HALF, 3], planes[3][:].indirect(offs_t[:, : HALF // 16]))
+        nc.scalar.activation(grouped[:, HALF:, 3], last_bf[:].indirect(offs_t[:, HALF // 16 :]), ACT.Copy)
+        nc.vector.tensor_scalar(rest_t[:], frac_t[:], -1.0, 1.0, ALU.mult, ALU.add)
+
+        for i in range(S // PIECE):
+            cols = slice(i * PIECE, (i + 1) * PIECE)
+            codes = keep.tile([P, PIECE], U32, name="codes%d" % i, align_bytes=64)
+            scales = keep.tile([P, PIECE], U8, name="scales%d" % i, align_bytes=64)
+            acc = psum.tile([P, PIECE], F32, name="acc%d" % i)
+            nc.vector.quantize_mx(
+                out=codes[:].bitcast(FP8X4),
+                scales=scales[:],
+                in_=grouped[:, cols, :].rearrange("p c t -> p (c t)"),
+            )
+            nc.tensor.matmul_mx(
+                out=acc[:],
+                lhsT=w_words[:].bitcast(FP4X4),
+                lhsT_scale=w_scales[:],
+                rhs=codes[:].bitcast(FP8X4),
+                rhs_scale=scales[:],
+                start=True,
+                stop=True,
+            )
+            nc.scalar.activation(y[:, cols], acc[:], ACT.Gelu_apprx_tanh)
+
+        lo = keep.tile([P, V], F32, name="lo")
+        hi = keep.tile([P, V], F32, name="hi")
+        res = keep.tile([P, V], F32, name="res")
+
+        def weighted(dst, lst, weight, a, b):
+            nc.vector.tensor_tensor(dst[:, a:b], y[:].indirect(lst[:, a // 16 : b // 16]), weight[:, a:b], ALU.mult)
+
+        def finish(a, b):
+            nc.vector.tensor_tensor(res[:, a:b], lo[:, a:b], hi[:, a:b], ALU.add)
+
+        weighted(hi, right_t, frac_t, 0, 256)
+        weighted(lo, left_t, rest_t, 0, 256)
+        weighted(hi, right_t, frac_t, 256, 512)
+        finish(0, 256)
+        nc.sync.dma_start(out[:, 0:256], res[:, 0:256])
+        weighted(lo, left_t, rest_t, 256, 384)
+        weighted(lo, left_t, rest_t, 384, 512)
+        finish(256, 384)
+        nc.scalar.dma_start(out[:, 256:384], res[:, 256:384])
+        finish(384, 512)
+        nc.sync.dma_start(out[:, 384:512], res[:, 384:512])

@@ -19,9 +19,9 @@ ALU = mybir.AluOpType
 P = 128
 PACK = 4
 HALF = S // 2
-PIECE = 256
-LAST_CHUNKS = (1024, 1024, 1024, 768, 256)
-VECTOR_CHUNK = 3
+PIECES = (256, 256, 256, 256)
+LAST_CHUNKS = (1024, 1024, 1024, 512, 512)
+VECTOR_CHUNK = 2
 
 
 def tile_picked_lerp_gelu_e_kernel(tc, xT, w1_words, w1_scales, frac, offs, left, right, out):
@@ -48,6 +48,13 @@ def tile_picked_lerp_gelu_e_kernel(tc, xT, w1_words, w1_scales, frac, offs, left
         nc.scalar.activation(warm_out[:], warm_in[:], ACT.Gelu_apprx_tanh)
         nc.vector.memset(w_scales[:].bitcast(I32), 0)
 
+        nc.scalar.dma_start(w_words[:].bitcast(I32), w1_words[0].bitcast(I32))
+        for q in range(4):
+            nc.scalar.dma_start(
+                w_scales[32 * q : 32 * q + 4, :].bitcast(I32),
+                w1_scales[0, 4 * q : 4 * q + 4, :].bitcast(I32),
+            )
+
         rows = xT.rearrange("(p j) c -> p j c", j=PACK)
         nc.sync.dma_start(planes[0][:], rows[:, 0, :])
         nc.sync.dma_start(offs_t[:], offs)
@@ -60,12 +67,6 @@ def tile_picked_lerp_gelu_e_kernel(tc, xT, w1_words, w1_scales, frac, offs, left
             c0 = c0 + width
         for cols in spans:
             nc.sync.dma_start(planes[3][:, cols], rows[:, 3, cols])
-        nc.sync.dma_start(w_words[:].bitcast(I32), w1_words[0].bitcast(I32))
-        for q in range(4):
-            nc.sync.dma_start(
-                w_scales[32 * q : 32 * q + 4, :].bitcast(I32),
-                w1_scales[0, 4 * q : 4 * q + 4, :].bitcast(I32),
-            )
         nc.sync.dma_start(frac_t[:], frac)
         nc.sync.dma_start(left_t[:], left)
         nc.sync.dma_start(right_t[:], right)
@@ -81,11 +82,11 @@ def tile_picked_lerp_gelu_e_kernel(tc, xT, w1_words, w1_scales, frac, offs, left
         nc.scalar.activation(grouped[:, HALF:, 3], last_bf[:].indirect(offs_t[:, HALF // 16 :]), ACT.Copy)
         nc.vector.tensor_scalar(rest_t[:], frac_t[:], -1.0, 1.0, ALU.mult, ALU.add)
 
-        for i in range(S // PIECE):
-            cols = slice(i * PIECE, (i + 1) * PIECE)
-            codes = keep.tile([P, PIECE], U32, name="codes%d" % i, align_bytes=64)
-            scales = keep.tile([P, PIECE], U8, name="scales%d" % i, align_bytes=64)
-            acc = psum.tile([P, PIECE], F32, name="acc%d" % i)
+        for i, width in enumerate(PIECES):
+            cols = slice(sum(PIECES[:i]), sum(PIECES[: i + 1]))
+            codes = keep.tile([P, width], U32, name="codes%d" % i, align_bytes=64)
+            scales = keep.tile([P, width], U8, name="scales%d" % i, align_bytes=64)
+            acc = psum.tile([P, width], F32, name="acc%d" % i)
             nc.vector.quantize_mx(
                 out=codes[:].bitcast(FP8X4),
                 scales=scales[:],
@@ -112,14 +113,10 @@ def tile_picked_lerp_gelu_e_kernel(tc, xT, w1_words, w1_scales, frac, offs, left
         def finish(a, b):
             nc.vector.tensor_tensor(res[:, a:b], lo[:, a:b], hi[:, a:b], ALU.add)
 
-        weighted(hi, right_t, frac_t, 0, 256)
+        weighted(hi, right_t, frac_t, 0, 512)
         weighted(lo, left_t, rest_t, 0, 256)
-        weighted(hi, right_t, frac_t, 256, 512)
+        weighted(lo, left_t, rest_t, 256, 512)
         finish(0, 256)
-        nc.sync.dma_start(out[:, 0:256], res[:, 0:256])
-        weighted(lo, left_t, rest_t, 256, 384)
-        weighted(lo, left_t, rest_t, 384, 512)
-        finish(256, 384)
-        nc.scalar.dma_start(out[:, 256:384], res[:, 256:384])
-        finish(384, 512)
-        nc.sync.dma_start(out[:, 384:512], res[:, 384:512])
+        nc.scalar.dma_start(out[:, 0:256], res[:, 0:256])
+        finish(256, 512)
+        nc.sync.dma_start(out[:, 256:512], res[:, 256:512])

@@ -20,8 +20,8 @@ P = 128
 PACK = 4
 HALF = S // 2
 PIECES = (256, 256, 256, 256)
-LAST_CHUNKS = (1024, 1024, 1024, 512, 512)
-VECTOR_CHUNK = 2
+LAST_CHUNKS = (1024, 1024, 1024, 768, 256)
+VECTOR_SHARES = (0, 0, 256, 512, 0)
 
 
 def tile_picked_lerp_gelu_e_kernel(tc, xT, w1_words, w1_scales, frac, offs, left, right, out):
@@ -39,7 +39,6 @@ def tile_picked_lerp_gelu_e_kernel(tc, xT, w1_words, w1_scales, frac, offs, left
         w_words = keep.tile([P, 2 * N], U8, name="w_words", align_bytes=64)
         w_scales = keep.tile([P, N], U8, name="w_scales", align_bytes=64)
         frac_t = keep.tile([P, V], F32, name="frac_t")
-        rest_t = keep.tile([P, V], F32, name="rest_t")
         y = keep.tile([P, S], F32, name="y")
         warm_in = keep.tile([P, 8], F32, name="warm_in")
         warm_out = keep.tile([P, 8], F32, name="warm_out")
@@ -47,13 +46,6 @@ def tile_picked_lerp_gelu_e_kernel(tc, xT, w1_words, w1_scales, frac, offs, left
         nc.gpsimd.memset(warm_in[:], 0.0)
         nc.scalar.activation(warm_out[:], warm_in[:], ACT.Gelu_apprx_tanh)
         nc.vector.memset(w_scales[:].bitcast(I32), 0)
-
-        nc.scalar.dma_start(w_words[:].bitcast(I32), w1_words[0].bitcast(I32))
-        for q in range(4):
-            nc.scalar.dma_start(
-                w_scales[32 * q : 32 * q + 4, :].bitcast(I32),
-                w1_scales[0, 4 * q : 4 * q + 4, :].bitcast(I32),
-            )
 
         rows = xT.rearrange("(p j) c -> p j c", j=PACK)
         nc.sync.dma_start(planes[0][:], rows[:, 0, :])
@@ -67,20 +59,26 @@ def tile_picked_lerp_gelu_e_kernel(tc, xT, w1_words, w1_scales, frac, offs, left
             c0 = c0 + width
         for cols in spans:
             nc.sync.dma_start(planes[3][:, cols], rows[:, 3, cols])
+        nc.sync.dma_start(w_words[:].bitcast(I32), w1_words[0].bitcast(I32))
+        for q in range(4):
+            nc.sync.dma_start(
+                w_scales[32 * q : 32 * q + 4, :].bitcast(I32),
+                w1_scales[0, 4 * q : 4 * q + 4, :].bitcast(I32),
+            )
         nc.sync.dma_start(frac_t[:], frac)
-        nc.sync.dma_start(left_t[:], left)
         nc.sync.dma_start(right_t[:], right)
+        nc.sync.dma_start(left_t[:], left)
 
         for t in range(PACK - 1):
             nc.vector.tensor_copy(grouped[:, :, t], planes[t][:].indirect(offs_t[:]))
-        for i, cols in enumerate(spans):
-            if i == VECTOR_CHUNK:
-                nc.vector.tensor_copy(last_bf[:, cols], planes[3][:, cols])
-            else:
-                nc.scalar.activation(last_bf[:, cols], planes[3][:, cols], ACT.Copy)
+        for cols, share in zip(spans, VECTOR_SHARES):
+            mine = slice(cols.start, cols.start + share)
+            other = slice(cols.start + share, cols.stop)
+            if share:
+                nc.vector.tensor_copy(last_bf[:, mine], planes[3][:, mine])
+            nc.scalar.activation(last_bf[:, other], planes[3][:, other], ACT.Copy)
         nc.vector.tensor_copy(grouped[:, :HALF, 3], planes[3][:].indirect(offs_t[:, : HALF // 16]))
         nc.scalar.activation(grouped[:, HALF:, 3], last_bf[:].indirect(offs_t[:, HALF // 16 :]), ACT.Copy)
-        nc.vector.tensor_scalar(rest_t[:], frac_t[:], -1.0, 1.0, ALU.mult, ALU.add)
 
         for i, width in enumerate(PIECES):
             cols = slice(sum(PIECES[:i]), sum(PIECES[: i + 1]))
@@ -102,6 +100,9 @@ def tile_picked_lerp_gelu_e_kernel(tc, xT, w1_words, w1_scales, frac, offs, left
                 stop=True,
             )
             nc.scalar.activation(y[:, cols], acc[:], ACT.Gelu_apprx_tanh)
+
+        rest_t = grouped[:, S - PIECES[-1] :, :].rearrange("p c t -> p (c t)").bitcast(F32)
+        nc.vector.tensor_scalar(rest_t, frac_t[:], -1.0, 1.0, ALU.mult, ALU.add)
 
         lo = keep.tile([P, V], F32, name="lo")
         hi = keep.tile([P, V], F32, name="hi")

@@ -19,7 +19,7 @@ ALU = mybir.AluOpType
 P = 128
 PACK = 4
 HALF = S // 2
-PIECES = (256, 256, 256, 256)
+PIECES = (128,) * 8
 LAST_CHUNKS = (1024, 1024, 1024, 768, 256)
 VECTOR_SHARES = (0, 0, 256, 512, 0)
 
@@ -101,7 +101,7 @@ def tile_picked_lerp_gelu_e_kernel(tc, xT, w1_words, w1_scales, frac, offs, left
             )
             nc.scalar.activation(y[:, cols], acc[:], ACT.Gelu_apprx_tanh)
 
-        rest_t = grouped[:, S - PIECES[-1] :, :].rearrange("p c t -> p (c t)").bitcast(F32)
+        rest_t = grouped[:, S - V // 2 :, :].rearrange("p c t -> p (c t)").bitcast(F32)
         nc.vector.tensor_scalar(rest_t, frac_t[:], -1.0, 1.0, ALU.mult, ALU.add)
 
         lo = keep.tile([P, V], F32, name="lo")

@@ -20,8 +20,8 @@ P = 128
 PACK = 4
 HALF = S // 2
 PIECES = (128,) * 8
-LAST_CHUNKS = (1024, 1024, 1024, 768, 256)
-VECTOR_SHARES = (0, 0, 256, 512, 0)
+LAST_CHUNKS = (1024, 1024, 1152, 640, 256)
+VECTOR_SHARES = (0, 0, 576, 256, 0)
 
 
 def tile_picked_lerp_gelu_e_kernel(tc, xT, w1_words, w1_scales, frac, offs, left, right, out):

@@ -20,7 +20,7 @@ P = 128
 PACK = 4
 HALF = S // 2
 PIECES = (128,) * 8
-LAST_CHUNKS = (1024, 1024, 1152, 640, 256)
+LAST_CHUNKS = (1088, 1152, 1152, 512, 192)
 VECTOR_SHARES = (0, 0, 576, 256, 0)
 
 
@@ -47,6 +47,13 @@ def tile_picked_lerp_gelu_e_kernel(tc, xT, w1_words, w1_scales, frac, offs, left
         nc.scalar.activation(warm_out[:], warm_in[:], ACT.Gelu_apprx_tanh)
         nc.vector.memset(w_scales[:].bitcast(I32), 0)
 
+        nc.scalar.dma_start(w_words[:].bitcast(I32), w1_words[0].bitcast(I32))
+        for q in range(4):
+            nc.scalar.dma_start(
+                w_scales[32 * q : 32 * q + 4, :].bitcast(I32),
+                w1_scales[0, 4 * q : 4 * q + 4, :].bitcast(I32),
+            )
+
         rows = xT.rearrange("(p j) c -> p j c", j=PACK)
         nc.sync.dma_start(planes[0][:], rows[:, 0, :])
         nc.sync.dma_start(offs_t[:], offs)
@@ -59,12 +66,6 @@ def tile_picked_lerp_gelu_e_kernel(tc, xT, w1_words, w1_scales, frac, offs, left
             c0 = c0 + width
         for cols in spans:
             nc.sync.dma_start(planes[3][:, cols], rows[:, 3, cols])
-        nc.sync.dma_start(w_words[:].bitcast(I32), w1_words[0].bitcast(I32))
-        for q in range(4):
-            nc.sync.dma_start(
-                w_scales[32 * q : 32 * q + 4, :].bitcast(I32),
-                w1_scales[0, 4 * q : 4 * q + 4, :].bitcast(I32),
-            )
         nc.sync.dma_start(frac_t[:], frac)
         nc.sync.dma_start(right_t[:], right)
         nc.sync.dma_start(left_t[:], left)

@@ -20,8 +20,8 @@ P = 128
 PACK = 4
 HALF = S // 2
 PIECES = (128,) * 8
-LAST_CHUNKS = (1088, 1152, 1152, 512, 192)
-VECTOR_SHARES = (0, 0, 576, 256, 0)
+LAST_CHUNKS = (2368, 1280, 384, 64)
+VECTOR_SHARES = (1088, 832, 256, 0)
 
 
 def tile_picked_lerp_gelu_e_kernel(tc, xT, w1_words, w1_scales, frac, offs, left, right, out):

@@ -105,20 +105,18 @@ def tile_picked_lerp_gelu_e_kernel(tc, xT, w1_words, w1_scales, frac, offs, left
         rest_t = grouped[:, S - V // 2 :, :].rearrange("p c t -> p (c t)").bitcast(F32)
         nc.vector.tensor_scalar(rest_t, frac_t[:], -1.0, 1.0, ALU.mult, ALU.add)
 
+        picked = keep.tile([P, V], F32, name="picked")
         lo = keep.tile([P, V], F32, name="lo")
         hi = keep.tile([P, V], F32, name="hi")
         res = keep.tile([P, V], F32, name="res")
 
-        def weighted(dst, lst, weight, a, b):
-            nc.vector.tensor_tensor(dst[:, a:b], y[:].indirect(lst[:, a // 16 : b // 16]), weight[:, a:b], ALU.mult)
-
-        def finish(a, b):
-            nc.vector.tensor_tensor(res[:, a:b], lo[:, a:b], hi[:, a:b], ALU.add)
-
-        weighted(hi, right_t, frac_t, 0, 512)
-        weighted(lo, left_t, rest_t, 0, 256)
-        weighted(lo, left_t, rest_t, 256, 512)
-        finish(0, 256)
-        nc.scalar.dma_start(out[:, 0:256], res[:, 0:256])
-        finish(256, 512)
-        nc.sync.dma_start(out[:, 256:512], res[:, 256:512])
+        halves = (slice(0, V // 2), slice(V // 2, V))
+        for cols in halves:
+            entries = left_t[:, cols.start // 16 : cols.stop // 16]
+            nc.scalar.activation(picked[:, cols], y[:].indirect(entries), ACT.Copy)
+        nc.vector.tensor_tensor(hi[:], y[:].indirect(right_t[:]), frac_t[:], ALU.mult)
+        for cols in halves:
+            nc.vector.tensor_tensor(lo[:, cols], picked[:, cols], rest_t[:, cols], ALU.mult)
+        for cols, queue in zip(halves, (nc.scalar, nc.sync)):
+            nc.vector.tensor_tensor(res[:, cols], lo[:, cols], hi[:, cols], ALU.add)
+            queue.dma_start(out[:, cols], res[:, cols])

@@ -20,8 +20,7 @@ P = 128
 PACK = 4
 HALF = S // 2
 PIECES = (128,) * 8
-LAST_CHUNKS = (2368, 1280, 384, 64)
-VECTOR_SHARES = (1088, 832, 256, 0)
+PIECE = 128
 
 
 def tile_picked_lerp_gelu_e_kernel(tc, xT, w1_words, w1_scales, frac, offs, left, right, out):
@@ -34,7 +33,6 @@ def tile_picked_lerp_gelu_e_kernel(tc, xT, w1_words, w1_scales, frac, offs, left
         left_t = keep.tile([P, V // 16], U16, name="left_t")
         right_t = keep.tile([P, V // 16], U16, name="right_t")
         planes = [keep.tile([P, T], F32, name="plane%d" % t) for t in range(PACK)]
-        last_bf = keep.tile([P, T], BF16, name="last_bf")
         grouped = keep.tile([P, S, PACK], BF16, name="grouped", align_bytes=64)
         w_words = keep.tile([P, 2 * N], U8, name="w_words", align_bytes=64)
         w_scales = keep.tile([P, N], U8, name="w_scales", align_bytes=64)
@@ -59,27 +57,23 @@ def tile_picked_lerp_gelu_e_kernel(tc, xT, w1_words, w1_scales, frac, offs, left
         nc.sync.dma_start(offs_t[:], offs)
         nc.sync.dma_start(planes[1][:], rows[:, 1, :])
         nc.sync.dma_start(planes[2][:], rows[:, 2, :])
-        spans = []
-        c0 = 0
-        for width in LAST_CHUNKS:
-            spans.append(slice(c0, c0 + width))
-            c0 = c0 + width
-        for cols in spans:
-            nc.sync.dma_start(planes[3][:, cols], rows[:, 3, cols])
+        nc.sync.dma_start(planes[3][:], rows[:, 3, :])
         nc.sync.dma_start(frac_t[:], frac)
         nc.sync.dma_start(right_t[:], right)
         nc.sync.dma_start(left_t[:], left)
 
-        for t in range(PACK - 1):
+        for t in range(2):
             nc.vector.tensor_copy(grouped[:, :, t], planes[t][:].indirect(offs_t[:]))
-        for cols, share in zip(spans, VECTOR_SHARES):
-            mine = slice(cols.start, cols.start + share)
-            other = slice(cols.start + share, cols.stop)
-            if share:
-                nc.vector.tensor_copy(last_bf[:, mine], planes[3][:, mine])
-            nc.scalar.activation(last_bf[:, other], planes[3][:, other], ACT.Copy)
-        nc.vector.tensor_copy(grouped[:, :HALF, 3], planes[3][:].indirect(offs_t[:, : HALF // 16]))
-        nc.scalar.activation(grouped[:, HALF:, 3], last_bf[:].indirect(offs_t[:, HALF // 16 :]), ACT.Copy)
+        cut = HALF - PIECE
+        for t in range(2, PACK):
+            loose = keep.tile([P, HALF], BF16, name="loose%d" % t)
+            nc.vector.tensor_copy(grouped[:, :HALF, t], planes[t][:].indirect(offs_t[:, : HALF // 16]))
+            for a, b in ((cut, HALF), (0, PIECE), (PIECE, cut)):
+                entries = offs_t[:, (HALF + a) // 16 : (HALF + b) // 16]
+                nc.scalar.activation(loose[:, a:b], planes[t][:].indirect(entries), ACT.Copy)
+            nc.vector.tensor_copy(grouped[:, HALF + cut :, t], loose[:, cut:])
+            for a in range(0, cut, PIECE):
+                nc.scalar.copy(grouped[:, HALF + a : HALF + a + PIECE, t], loose[:, a : a + PIECE])
 
         for i, width in enumerate(PIECES):
             cols = slice(sum(PIECES[:i]), sum(PIECES[: i + 1]))

@@ -32,7 +32,9 @@ def tile_picked_lerp_gelu_e_kernel(tc, xT, w1_words, w1_scales, frac, offs, left
         offs_t = keep.tile([P, S // 16], U16, name="offs_t")
         left_t = keep.tile([P, V // 16], U16, name="left_t")
         right_t = keep.tile([P, V // 16], U16, name="right_t")
-        planes = [keep.tile([P, T], F32, name="plane%d" % t) for t in range(PACK)]
+        first_two = keep.tile([P, 2 * T], F32, name="first_two")
+        planes = [first_two[:, :T], first_two[:, T:]]
+        planes.extend(keep.tile([P, T], F32, name="plane%d" % t)[:] for t in range(2, PACK))
         grouped = keep.tile([P, S, PACK], BF16, name="grouped", align_bytes=64)
         w_words = keep.tile([P, 2 * N], U8, name="w_words", align_bytes=64)
         w_scales = keep.tile([P, N], U8, name="w_scales", align_bytes=64)
@@ -53,24 +55,21 @@ def tile_picked_lerp_gelu_e_kernel(tc, xT, w1_words, w1_scales, frac, offs, left
             )
 
         rows = xT.rearrange("(p j) c -> p j c", j=PACK)
-        nc.sync.dma_start(planes[0][:], rows[:, 0, :])
+        nc.sync.dma_start(first_two[:], rows[:, 0:2, :].rearrange("p j c -> p (j c)"))
         nc.sync.dma_start(offs_t[:], offs)
-        nc.sync.dma_start(planes[1][:], rows[:, 1, :])
-        nc.sync.dma_start(planes[2][:], rows[:, 2, :])
-        nc.sync.dma_start(planes[3][:], rows[:, 3, :])
+        nc.sync.dma_start(planes[2], rows[:, 2, :])
+        nc.sync.dma_start(planes[3], rows[:, 3, :])
         nc.sync.dma_start(frac_t[:], frac)
         nc.sync.dma_start(right_t[:], right)
         nc.sync.dma_start(left_t[:], left)
 
-        for t in range(2):
-            nc.vector.tensor_copy(grouped[:, :, t], planes[t][:].indirect(offs_t[:]))
         cut = HALF - PIECE
-        for t in range(2, PACK):
-            loose = keep.tile([P, HALF], BF16, name="loose%d" % t)
-            nc.vector.tensor_copy(grouped[:, :HALF, t], planes[t][:].indirect(offs_t[:, : HALF // 16]))
+        for t in range(PACK):
+            loose = keep.tile([P, HALF], F32 if t < 2 else BF16, name="loose%d" % t)
+            nc.vector.tensor_copy(grouped[:, :HALF, t], planes[t].indirect(offs_t[:, : HALF // 16]))
             for a, b in ((cut, HALF), (0, PIECE), (PIECE, cut)):
                 entries = offs_t[:, (HALF + a) // 16 : (HALF + b) // 16]
-                nc.scalar.activation(loose[:, a:b], planes[t][:].indirect(entries), ACT.Copy)
+                nc.scalar.activation(loose[:, a:b], planes[t].indirect(entries), ACT.Copy)
             nc.vector.tensor_copy(grouped[:, HALF + cut :, t], loose[:, cut:])
             for a in range(0, cut, PIECE):
                 nc.scalar.copy(grouped[:, HALF + a : HALF + a + PIECE, t], loose[:, a : a + PIECE])

@@ -18,9 +18,10 @@ ALU = mybir.AluOpType
 
 P = 128
 PACK = 4
-HALF = S // 2
-PIECES = (128,) * 8
 PIECE = 128
+HALF = S // 2
+POOL_FROM = S - 128
+EARLY_VECTOR = 768
 
 
 def tile_picked_lerp_gelu_e_kernel(tc, xT, w1_words, w1_scales, frac, offs, left, right, out):
@@ -46,41 +47,53 @@ def tile_picked_lerp_gelu_e_kernel(tc, xT, w1_words, w1_scales, frac, offs, left
         nc.gpsimd.memset(warm_in[:], 0.0)
         nc.scalar.activation(warm_out[:], warm_in[:], ACT.Gelu_apprx_tanh)
         nc.vector.memset(w_scales[:].bitcast(I32), 0)
-
         nc.scalar.dma_start(w_words[:].bitcast(I32), w1_words[0].bitcast(I32))
-        for q in range(4):
-            nc.scalar.dma_start(
-                w_scales[32 * q : 32 * q + 4, :].bitcast(I32),
-                w1_scales[0, 4 * q : 4 * q + 4, :].bitcast(I32),
-            )
 
         rows = xT.rearrange("(p j) c -> p j c", j=PACK)
         nc.sync.dma_start(first_two[:], rows[:, 0:2, :].rearrange("p j c -> p (j c)"))
         nc.sync.dma_start(offs_t[:], offs)
         nc.sync.dma_start(planes[2], rows[:, 2, :])
         nc.sync.dma_start(planes[3], rows[:, 3, :])
+        for q in range(4):
+            nc.sync.dma_start(
+                w_scales[32 * q : 32 * q + 4, :].bitcast(I32),
+                w1_scales[0, 4 * q : 4 * q + 4, :].bitcast(I32),
+            )
         nc.sync.dma_start(frac_t[:], frac)
         nc.sync.dma_start(right_t[:], right)
         nc.sync.dma_start(left_t[:], left)
 
-        cut = HALF - PIECE
-        for t in range(PACK):
-            loose = keep.tile([P, HALF], F32 if t < 2 else BF16, name="loose%d" % t)
-            nc.vector.tensor_copy(grouped[:, :HALF, t], planes[t].indirect(offs_t[:, : HALF // 16]))
-            for a, b in ((cut, HALF), (0, PIECE), (PIECE, cut)):
-                entries = offs_t[:, (HALF + a) // 16 : (HALF + b) // 16]
-                nc.scalar.activation(loose[:, a:b], planes[t].indirect(entries), ACT.Copy)
-            nc.vector.tensor_copy(grouped[:, HALF + cut :, t], loose[:, cut:])
-            for a in range(0, cut, PIECE):
-                nc.scalar.copy(grouped[:, HALF + a : HALF + a + PIECE, t], loose[:, a : a + PIECE])
+        def entries(a, b):
+            return offs_t[:, a // 16 : b // 16]
 
-        for i, width in enumerate(PIECES):
-            cols = slice(sum(PIECES[:i]), sum(PIECES[: i + 1]))
-            codes = keep.tile([P, width], U32, name="codes%d" % i, align_bytes=64)
-            scales = keep.tile([P, width], U8, name="scales%d" % i, align_bytes=64)
-            acc = psum.tile([P, width], F32, name="acc%d" % i)
+        def fetch(t, a, b, tag):
+            loose = keep.tile([P, b - a], F32 if t < 2 else BF16, name="loose", tag=tag, align_bytes=64)
+            nc.scalar.activation(loose[:], planes[t].indirect(entries(a, b)), ACT.Copy)
+            return loose
+
+        for t in range(PACK):
+            mine = EARLY_VECTOR if t < 2 else HALF
+            nc.vector.tensor_copy(grouped[:, :mine, t], planes[t].indirect(entries(0, mine)))
+            for_pool = fetch(t, POOL_FROM, S, "for_pool%d" % t)
+            nc.gpsimd.tensor_copy(grouped[:, POOL_FROM:, t], for_pool[:])
+            head = fetch(t, mine, mine + PIECE, "head%d" % t)
+            if mine + PIECE < POOL_FROM:
+                tail = fetch(t, mine + PIECE, POOL_FROM, "tail%d" % t)
+            nc.scalar.copy(grouped[:, mine : mine + PIECE, t], head[:])
+            for a in range(mine + PIECE, POOL_FROM, PIECE):
+                nc.scalar.copy(grouped[:, a : a + PIECE, t], tail[:, a - mine - PIECE : a - mine])
+
+        early_codes = keep.tile([P, HALF], U32, name="early_codes", tag="head3", align_bytes=64)
+        for i in (7, 4, 0, 1, 2, 3, 5, 6):
+            cols = slice(i * PIECE, (i + 1) * PIECE)
+            if cols.start < HALF:
+                codes = early_codes[:, cols]
+            else:
+                codes = keep.tile([P, PIECE], U32, name="codes%d" % i, align_bytes=64)[:]
+            scales = keep.tile([P, PIECE], U8, name="scales%d" % i, align_bytes=64)
+            acc = psum.tile([P, PIECE], F32, name="acc%d" % i)
             nc.vector.quantize_mx(
-                out=codes[:].bitcast(FP8X4),
+                out=codes.bitcast(FP8X4),
                 scales=scales[:],
                 in_=grouped[:, cols, :].rearrange("p c t -> p (c t)"),
             )
@@ -88,14 +101,14 @@ def tile_picked_lerp_gelu_e_kernel(tc, xT, w1_words, w1_scales, frac, offs, left
                 out=acc[:],
                 lhsT=w_words[:].bitcast(FP4X4),
                 lhsT_scale=w_scales[:],
-                rhs=codes[:].bitcast(FP8X4),
+                rhs=codes.bitcast(FP8X4),
                 rhs_scale=scales[:],
                 start=True,
                 stop=True,
             )
             nc.scalar.activation(y[:, cols], acc[:], ACT.Gelu_apprx_tanh)
 
-        rest_t = grouped[:, S - V // 2 :, :].rearrange("p c t -> p (c t)").bitcast(F32)
+        rest_t = grouped[:, 5 * PIECE : 7 * PIECE, :].rearrange("p c t -> p (c t)").bitcast(F32)
         nc.vector.tensor_scalar(rest_t, frac_t[:], -1.0, 1.0, ALU.mult, ALU.add)
 
         picked = keep.tile([P, V], F32, name="picked")
@@ -105,8 +118,7 @@ def tile_picked_lerp_gelu_e_kernel(tc, xT, w1_words, w1_scales, frac, offs, left
 
         halves = (slice(0, V // 2), slice(V // 2, V))
         for cols in halves:
-            entries = left_t[:, cols.start // 16 : cols.stop // 16]
-            nc.scalar.activation(picked[:, cols], y[:].indirect(entries), ACT.Copy)
+            nc.scalar.activation(picked[:, cols], y[:].indirect(left_t[:, cols.start // 16 : cols.stop // 16]), ACT.Copy)
         nc.vector.tensor_tensor(hi[:], y[:].indirect(right_t[:]), frac_t[:], ALU.mult)
         for cols in halves:
             nc.vector.tensor_tensor(lo[:, cols], picked[:, cols], rest_t[:, cols], ALU.mult)

@@ -19,9 +19,10 @@ ALU = mybir.AluOpType
 P = 128
 PACK = 4
 PIECE = 128
+LEFT_FIRST = 320
 HALF = S // 2
-POOL_FROM = S - 128
-EARLY_VECTOR = 768
+POOL_FROM = S - 160
+VECTOR_FROM = POOL_FROM - 64
 
 
 def tile_picked_lerp_gelu_e_kernel(tc, xT, w1_words, w1_scales, frac, offs, left, right, out):
@@ -72,19 +73,20 @@ def tile_picked_lerp_gelu_e_kernel(tc, xT, w1_words, w1_scales, frac, offs, left
             return loose
 
         for t in range(PACK):
-            mine = EARLY_VECTOR if t < 2 else HALF
+            mine = POOL_FROM if t < 2 else HALF
             nc.vector.tensor_copy(grouped[:, :mine, t], planes[t].indirect(entries(0, mine)))
             for_pool = fetch(t, POOL_FROM, S, "for_pool%d" % t)
             nc.gpsimd.tensor_copy(grouped[:, POOL_FROM:, t], for_pool[:])
-            head = fetch(t, mine, mine + PIECE, "head%d" % t)
-            if mine + PIECE < POOL_FROM:
-                tail = fetch(t, mine + PIECE, POOL_FROM, "tail%d" % t)
-            nc.scalar.copy(grouped[:, mine : mine + PIECE, t], head[:])
-            for a in range(mine + PIECE, POOL_FROM, PIECE):
-                nc.scalar.copy(grouped[:, a : a + PIECE, t], tail[:, a - mine - PIECE : a - mine])
+            if t >= 2:
+                split = HALF + PIECE
+                head = fetch(t, HALF, split, "head%d" % t)
+                tail = fetch(t, split, POOL_FROM, "tail%d" % t)
+                nc.vector.tensor_copy(grouped[:, VECTOR_FROM:POOL_FROM, t], tail[:, VECTOR_FROM - split :])
+                nc.scalar.copy(grouped[:, HALF:split, t], head[:])
+                nc.scalar.copy(grouped[:, split:VECTOR_FROM, t], tail[:, : VECTOR_FROM - split])
 
-        early_codes = keep.tile([P, HALF], U32, name="early_codes", tag="head3", align_bytes=64)
-        for i in (7, 4, 0, 1, 2, 3, 5, 6):
+        early_codes = keep.tile([P, HALF], U32, name="early_codes", tag="for_pool3", align_bytes=64)
+        for i in (7, 0, 1, 2, 3, 4, 5, 6):
             cols = slice(i * PIECE, (i + 1) * PIECE)
             if cols.start < HALF:
                 codes = early_codes[:, cols]
@@ -116,12 +118,12 @@ def tile_picked_lerp_gelu_e_kernel(tc, xT, w1_words, w1_scales, frac, offs, left
         hi = keep.tile([P, V], F32, name="hi")
         res = keep.tile([P, V], F32, name="res")
 
-        halves = (slice(0, V // 2), slice(V // 2, V))
-        for cols in halves:
+        parts = (slice(0, LEFT_FIRST), slice(LEFT_FIRST, V))
+        for cols in parts:
             nc.scalar.activation(picked[:, cols], y[:].indirect(left_t[:, cols.start // 16 : cols.stop // 16]), ACT.Copy)
         nc.vector.tensor_tensor(hi[:], y[:].indirect(right_t[:]), frac_t[:], ALU.mult)
-        for cols in halves:
+        for cols in parts:
             nc.vector.tensor_tensor(lo[:, cols], picked[:, cols], rest_t[:, cols], ALU.mult)
-        for cols, queue in zip(halves, (nc.scalar, nc.sync)):
+        for cols, queue in zip((slice(0, V // 2), slice(V // 2, V)), (nc.scalar, nc.sync)):
             nc.vector.tensor_tensor(res[:, cols], lo[:, cols], hi[:, cols], ALU.add)
             queue.dma_start(out[:, cols], res[:, cols])

@@ -19,10 +19,11 @@ ALU = mybir.AluOpType
 P = 128
 PACK = 4
 PIECE = 128
+STORE_FIRST = 224
 LEFT_FIRST = 320
 HALF = S // 2
 POOL_FROM = S - 160
-VECTOR_FROM = POOL_FROM - 64
+VECTOR_FROM = POOL_FROM - 48
 
 
 def tile_picked_lerp_gelu_e_kernel(tc, xT, w1_words, w1_scales, frac, offs, left, right, out):
@@ -124,6 +125,6 @@ def tile_picked_lerp_gelu_e_kernel(tc, xT, w1_words, w1_scales, frac, offs, left
         nc.vector.tensor_tensor(hi[:], y[:].indirect(right_t[:]), frac_t[:], ALU.mult)
         for cols in parts:
             nc.vector.tensor_tensor(lo[:, cols], picked[:, cols], rest_t[:, cols], ALU.mult)
-        for cols, queue in zip((slice(0, V // 2), slice(V // 2, V)), (nc.scalar, nc.sync)):
+        for cols, queue in zip((slice(0, STORE_FIRST), slice(STORE_FIRST, V)), (nc.scalar, nc.sync)):
             nc.vector.tensor_tensor(res[:, cols], lo[:, cols], hi[:, cols], ALU.add)
             queue.dma_start(out[:, cols], res[:, cols])

@@ -50,17 +50,17 @@ def tile_picked_lerp_gelu_e_kernel(tc, xT, w1_words, w1_scales, frac, offs, left
         nc.scalar.activation(warm_out[:], warm_in[:], ACT.Gelu_apprx_tanh)
         nc.vector.memset(w_scales[:].bitcast(I32), 0)
         nc.scalar.dma_start(w_words[:].bitcast(I32), w1_words[0].bitcast(I32))
+        for q in range(4):
+            nc.scalar.dma_start(
+                w_scales[32 * q : 32 * q + 4, :].bitcast(I32),
+                w1_scales[0, 4 * q : 4 * q + 4, :].bitcast(I32),
+            )
 
         rows = xT.rearrange("(p j) c -> p j c", j=PACK)
         nc.sync.dma_start(first_two[:], rows[:, 0:2, :].rearrange("p j c -> p (j c)"))
         nc.sync.dma_start(offs_t[:], offs)
         nc.sync.dma_start(planes[2], rows[:, 2, :])
         nc.sync.dma_start(planes[3], rows[:, 3, :])
-        for q in range(4):
-            nc.sync.dma_start(
-                w_scales[32 * q : 32 * q + 4, :].bitcast(I32),
-                w1_scales[0, 4 * q : 4 * q + 4, :].bitcast(I32),
-            )
         nc.sync.dma_start(frac_t[:], frac)
         nc.sync.dma_start(right_t[:], right)
         nc.sync.dma_start(left_t[:], left)

@@ -22,8 +22,8 @@ PIECE = 128
 STORE_FIRST = 224
 LEFT_FIRST = 320
 HALF = S // 2
-POOL_FROM = S - 160
-VECTOR_FROM = POOL_FROM - 48
+POOL_FROM = S - PIECE
+VECTOR_TO = HALF + 64
 
 
 def tile_picked_lerp_gelu_e_kernel(tc, xT, w1_words, w1_scales, frac, offs, left, right, out):
@@ -69,7 +69,7 @@ def tile_picked_lerp_gelu_e_kernel(tc, xT, w1_words, w1_scales, frac, offs, left
             return offs_t[:, a // 16 : b // 16]
 
         def fetch(t, a, b, tag):
-            loose = keep.tile([P, b - a], F32 if t < 2 else BF16, name="loose", tag=tag, align_bytes=64)
+            loose = keep.tile([P, b - a], BF16 if t >= 2 and b - a >= PIECE else F32, name="loose", tag=tag, align_bytes=64)
             nc.scalar.activation(loose[:], planes[t].indirect(entries(a, b)), ACT.Copy)
             return loose
 
@@ -79,12 +79,13 @@ def tile_picked_lerp_gelu_e_kernel(tc, xT, w1_words, w1_scales, frac, offs, left
             for_pool = fetch(t, POOL_FROM, S, "for_pool%d" % t)
             nc.gpsimd.tensor_copy(grouped[:, POOL_FROM:, t], for_pool[:])
             if t >= 2:
-                split = HALF + PIECE
-                head = fetch(t, HALF, split, "head%d" % t)
+                split = POOL_FROM - PIECE
+                for_vector = fetch(t, HALF, VECTOR_TO, "for_vector%d" % t)
+                nc.vector.tensor_copy(grouped[:, HALF:VECTOR_TO, t], for_vector[:])
+                head = fetch(t, VECTOR_TO, split, "head%d" % t)
                 tail = fetch(t, split, POOL_FROM, "tail%d" % t)
-                nc.vector.tensor_copy(grouped[:, VECTOR_FROM:POOL_FROM, t], tail[:, VECTOR_FROM - split :])
-                nc.scalar.copy(grouped[:, HALF:split, t], head[:])
-                nc.scalar.copy(grouped[:, split:VECTOR_FROM, t], tail[:, : VECTOR_FROM - split])
+                nc.scalar.copy(grouped[:, VECTOR_TO:split, t], head[:])
+                nc.scalar.copy(grouped[:, split:POOL_FROM, t], tail[:])
 
         early_codes = keep.tile([P, HALF], U32, name="early_codes", tag="for_pool3", align_bytes=64)
         for i in (7, 0, 1, 2, 3, 4, 5, 6):

@@ -23,7 +23,8 @@ STORE_FIRST = 224
 LEFT_FIRST = 320
 HALF = S // 2
 POOL_FROM = S - PIECE
-VECTOR_TO = HALF + 64
+FETCH_TO = HALF + 64
+VECTOR_TO = HALF + 48
 
 
 def tile_picked_lerp_gelu_e_kernel(tc, xT, w1_words, w1_scales, frac, offs, left, right, out):
@@ -69,7 +70,7 @@ def tile_picked_lerp_gelu_e_kernel(tc, xT, w1_words, w1_scales, frac, offs, left
             return offs_t[:, a // 16 : b // 16]
 
         def fetch(t, a, b, tag):
-            loose = keep.tile([P, b - a], BF16 if t >= 2 and b - a >= PIECE else F32, name="loose", tag=tag, align_bytes=64)
+            loose = keep.tile([P, b - a], BF16 if t >= 2 else F32, name="loose", tag=tag, align_bytes=64)
             nc.scalar.activation(loose[:], planes[t].indirect(entries(a, b)), ACT.Copy)
             return loose
 
@@ -80,11 +81,13 @@ def tile_picked_lerp_gelu_e_kernel(tc, xT, w1_words, w1_scales, frac, offs, left
             nc.gpsimd.tensor_copy(grouped[:, POOL_FROM:, t], for_pool[:])
             if t >= 2:
                 split = POOL_FROM - PIECE
-                for_vector = fetch(t, HALF, VECTOR_TO, "for_vector%d" % t)
-                nc.vector.tensor_copy(grouped[:, HALF:VECTOR_TO, t], for_vector[:])
-                head = fetch(t, VECTOR_TO, split, "head%d" % t)
+                head = keep.tile([P, split - HALF], F32, name="head%d" % t, align_bytes=64)
+                for a, b in ((HALF, FETCH_TO), (FETCH_TO, split)):
+                    nc.scalar.activation(head[:, a - HALF : b - HALF], planes[t].indirect(entries(a, b)), ACT.Copy)
+                    if a == HALF:
+                        nc.vector.tensor_copy(grouped[:, HALF:VECTOR_TO, t], head[:, : VECTOR_TO - HALF])
                 tail = fetch(t, split, POOL_FROM, "tail%d" % t)
-                nc.scalar.copy(grouped[:, VECTOR_TO:split, t], head[:])
+                nc.scalar.copy(grouped[:, VECTOR_TO:split, t], head[:, VECTOR_TO - HALF :])
                 nc.scalar.copy(grouped[:, split:POOL_FROM, t], tail[:])
 
         early_codes = keep.tile([P, HALF], U32, name="early_codes", tag="for_pool3", align_bytes=64)

@@ -22,9 +22,9 @@ PIECE = 128
 STORE_FIRST = 224
 LEFT_FIRST = 320
 HALF = S // 2
-POOL_FROM = S - PIECE
-FETCH_TO = HALF + 64
-VECTOR_TO = HALF + 48
+POOL_FROM = S - 192
+POOL_FIRST = S - 64
+SCALAR_CUT = HALF + 192
 
 
 def tile_picked_lerp_gelu_e_kernel(tc, xT, w1_words, w1_scales, frac, offs, left, right, out):
@@ -70,50 +70,54 @@ def tile_picked_lerp_gelu_e_kernel(tc, xT, w1_words, w1_scales, frac, offs, left
             return offs_t[:, a // 16 : b // 16]
 
         def fetch(t, a, b, tag):
-            loose = keep.tile([P, b - a], BF16 if t >= 2 else F32, name="loose", tag=tag, align_bytes=64)
+            whole_tile_form = t >= 2 and b - a >= PIECE
+            loose = keep.tile([P, b - a], BF16 if whole_tile_form else F32, name="loose", tag=tag, align_bytes=64)
             nc.scalar.activation(loose[:], planes[t].indirect(entries(a, b)), ACT.Copy)
             return loose
 
+        last = PACK - 1
         for t in range(PACK):
             mine = POOL_FROM if t < 2 else HALF
             nc.vector.tensor_copy(grouped[:, :mine, t], planes[t].indirect(entries(0, mine)))
-            for_pool = fetch(t, POOL_FROM, S, "for_pool%d" % t)
-            nc.gpsimd.tensor_copy(grouped[:, POOL_FROM:, t], for_pool[:])
+            pool_parts = ((POOL_FIRST, S), (POOL_FROM, POOL_FIRST)) if t == last else ((POOL_FROM, S),)
+            for a, b in pool_parts:
+                nc.gpsimd.tensor_copy(grouped[:, a:b, t], fetch(t, a, b, "for_pool%d_%d" % (t, a))[:])
             if t >= 2:
-                split = POOL_FROM - PIECE
-                head = keep.tile([P, split - HALF], F32, name="head%d" % t, align_bytes=64)
-                for a, b in ((HALF, FETCH_TO), (FETCH_TO, split)):
-                    nc.scalar.activation(head[:, a - HALF : b - HALF], planes[t].indirect(entries(a, b)), ACT.Copy)
-                    if a == HALF:
-                        nc.vector.tensor_copy(grouped[:, HALF:VECTOR_TO, t], head[:, : VECTOR_TO - HALF])
-                tail = fetch(t, split, POOL_FROM, "tail%d" % t)
-                nc.scalar.copy(grouped[:, VECTOR_TO:split, t], head[:, VECTOR_TO - HALF :])
-                nc.scalar.copy(grouped[:, split:POOL_FROM, t], tail[:])
+                own = [(a, b, fetch(t, a, b, "own%d_%d" % (t, a))) for a, b in ((HALF, SCALAR_CUT), (SCALAR_CUT, POOL_FROM))]
+                for a, b, loose in own:
+                    nc.scalar.copy(grouped[:, a:b, t], loose[:])
 
-        early_codes = keep.tile([P, HALF], U32, name="early_codes", tag="for_pool3", align_bytes=64)
-        for i in (7, 0, 1, 2, 3, 4, 5, 6):
-            cols = slice(i * PIECE, (i + 1) * PIECE)
-            if cols.start < HALF:
-                codes = early_codes[:, cols]
-            else:
-                codes = keep.tile([P, PIECE], U32, name="codes%d" % i, align_bytes=64)[:]
-            scales = keep.tile([P, PIECE], U8, name="scales%d" % i, align_bytes=64)
+        all_codes = keep.tile([P, S], U32, name="all_codes", tag="for_pool%d_%d" % (last, POOL_FROM), align_bytes=64)
+        scales = keep.tile([P, S], U8, name="scales", align_bytes=64)
+
+        def codes(a, b):
+            return all_codes[:, a:b].bitcast(FP8X4)
+
+        def quantise(a, b):
+            nc.vector.quantize_mx(out=codes(a, b), scales=scales[:, a:b], in_=grouped[:, a:b, :].rearrange("p c t -> p (c t)"))
+
+        def project(i):
+            a, b = i * PIECE, (i + 1) * PIECE
             acc = psum.tile([P, PIECE], F32, name="acc%d" % i)
-            nc.vector.quantize_mx(
-                out=codes.bitcast(FP8X4),
-                scales=scales[:],
-                in_=grouped[:, cols, :].rearrange("p c t -> p (c t)"),
-            )
             nc.tensor.matmul_mx(
                 out=acc[:],
                 lhsT=w_words[:].bitcast(FP4X4),
                 lhsT_scale=w_scales[:],
-                rhs=codes.bitcast(FP8X4),
-                rhs_scale=scales[:],
+                rhs=codes(a, b),
+                rhs_scale=scales[:, a:b],
                 start=True,
                 stop=True,
             )
-            nc.scalar.activation(y[:, cols], acc[:], ACT.Gelu_apprx_tanh)
+            nc.scalar.activation(y[:, a:b], acc[:], ACT.Gelu_apprx_tanh)
+
+        quantise(7 * PIECE, S)
+        project(7)
+        quantise(POOL_FROM, 7 * PIECE)
+        for i in range(6):
+            quantise(i * PIECE, (i + 1) * PIECE)
+            project(i)
+        quantise(6 * PIECE, POOL_FROM)
+        project(6)
 
         rest_t = grouped[:, 5 * PIECE : 7 * PIECE, :].rearrange("p c t -> p (c t)").bitcast(F32)
         nc.vector.tensor_scalar(rest_t, frac_t[:], -1.0, 1.0, ALU.mult, ALU.add)

@@ -22,9 +22,10 @@ PIECE = 128
 STORE_FIRST = 224
 LEFT_FIRST = 320
 HALF = S // 2
-POOL_FROM = S - 192
+POOL_FROM = S - 160
+VECTOR_TO = HALF + 32
 POOL_FIRST = S - 64
-SCALAR_CUT = HALF + 192
+SCALAR_CUT = 6 * PIECE
 
 
 def tile_picked_lerp_gelu_e_kernel(tc, xT, w1_words, w1_scales, frac, offs, left, right, out):
@@ -79,15 +80,19 @@ def tile_picked_lerp_gelu_e_kernel(tc, xT, w1_words, w1_scales, frac, offs, left
         for t in range(PACK):
             mine = POOL_FROM if t < 2 else HALF
             nc.vector.tensor_copy(grouped[:, :mine, t], planes[t].indirect(entries(0, mine)))
-            pool_parts = ((POOL_FIRST, S), (POOL_FROM, POOL_FIRST)) if t == last else ((POOL_FROM, S),)
-            for a, b in pool_parts:
-                nc.gpsimd.tensor_copy(grouped[:, a:b, t], fetch(t, a, b, "for_pool%d_%d" % (t, a))[:])
-            if t >= 2:
-                own = [(a, b, fetch(t, a, b, "own%d_%d" % (t, a))) for a, b in ((HALF, SCALAR_CUT), (SCALAR_CUT, POOL_FROM))]
-                for a, b, loose in own:
-                    nc.scalar.copy(grouped[:, a:b, t], loose[:])
+            if t < 2:
+                nc.gpsimd.tensor_copy(grouped[:, POOL_FROM:, t], fetch(t, POOL_FROM, S, "for_pool%d" % t)[:])
+                continue
+            nc.gpsimd.tensor_copy(grouped[:, POOL_FIRST:, t], fetch(t, POOL_FIRST, S, "first%d" % t)[:])
+            nc.gpsimd.tensor_copy(grouped[:, POOL_FROM:POOL_FIRST, t], fetch(t, POOL_FROM, POOL_FIRST, "second%d" % t)[:])
+            head = fetch(t, HALF, SCALAR_CUT, "head%d" % t)
+            tail = fetch(t, SCALAR_CUT, POOL_FROM, "tail%d" % t)
+            if t < last:
+                nc.vector.tensor_copy(grouped[:, HALF:VECTOR_TO, t], head[:, : VECTOR_TO - HALF])
+            nc.scalar.copy(grouped[:, VECTOR_TO:SCALAR_CUT, t], head[:, VECTOR_TO - HALF :])
+            nc.scalar.copy(grouped[:, SCALAR_CUT:POOL_FROM, t], tail[:])
 
-        all_codes = keep.tile([P, S], U32, name="all_codes", tag="for_pool%d_%d" % (last, POOL_FROM), align_bytes=64)
+        all_codes = keep.tile([P, S], U32, name="all_codes", tag="second%d" % last, align_bytes=64)
         scales = keep.tile([P, S], U8, name="scales", align_bytes=64)
 
         def codes(a, b):
@@ -112,12 +117,10 @@ def tile_picked_lerp_gelu_e_kernel(tc, xT, w1_words, w1_scales, frac, offs, left
 
         quantise(7 * PIECE, S)
         project(7)
-        quantise(POOL_FROM, 7 * PIECE)
-        for i in range(6):
+        nc.vector.tensor_copy(grouped[:, HALF:VECTOR_TO, last], head[:, : VECTOR_TO - HALF])
+        for i in range(7):
             quantise(i * PIECE, (i + 1) * PIECE)
             project(i)
-        quantise(6 * PIECE, POOL_FROM)
-        project(6)
 
         rest_t = grouped[:, 5 * PIECE : 7 * PIECE, :].rearrange("p c t -> p (c t)").bitcast(F32)
         nc.vector.tensor_scalar(rest_t, frac_t[:], -1.0, 1.0, ALU.mult, ALU.add)

from contextlib import ExitStack

import concourse.mybir as mybir

K, T, S, V, N = 512, 4096, 1024, 512, 128
FLOPS = 2 * K * S * N

F32 = mybir.dt.float32
BF16 = mybir.dt.bfloat16
I32 = mybir.dt.int32
U32 = mybir.dt.uint32
U16 = mybir.dt.uint16
U8 = mybir.dt.uint8
FP8X4 = mybir.dt.float8_e4m3fn_x4
FP4X4 = mybir.dt.float4_e2m1fn_x4
ACT = mybir.ActivationFunctionType
ALU = mybir.AluOpType

P = 128
PACK = 4
PIECE = 128
STORE_FIRST = 224
LEFT_FIRST = 320
HALF = S // 2
POOL_FROM = S - 160
VECTOR_TO = HALF + 32
POOL_FIRST = S - 64
SCALAR_CUT = 6 * PIECE


def tile_picked_lerp_gelu_e_kernel(tc, xT, w1_words, w1_scales, frac, offs, left, right, out):
    nc = tc.nc
    with ExitStack() as ctx:
        keep = ctx.enter_context(tc.tile_pool(name="keep", bufs=1))
        psum = ctx.enter_context(tc.psum_pool(name="psum", bufs=1))

        offs_t = keep.tile([P, S // 16], U16, name="offs_t")
        left_t = keep.tile([P, V // 16], U16, name="left_t")
        right_t = keep.tile([P, V // 16], U16, name="right_t")
        first_two = keep.tile([P, 2 * T], F32, name="first_two")
        planes = [first_two[:, :T], first_two[:, T:]]
        planes.extend(keep.tile([P, T], F32, name="plane%d" % t)[:] for t in range(2, PACK))
        grouped = keep.tile([P, S, PACK], BF16, name="grouped", align_bytes=64)
        w_words = keep.tile([P, 2 * N], U8, name="w_words", align_bytes=64)
        w_scales = keep.tile([P, N], U8, name="w_scales", align_bytes=64)
        frac_t = keep.tile([P, V], F32, name="frac_t")
        y = keep.tile([P, S], F32, name="y")
        warm_in = keep.tile([P, 8], F32, name="warm_in")
        warm_out = keep.tile([P, 8], F32, name="warm_out")

        nc.gpsimd.memset(warm_in[:], 0.0)
        nc.scalar.activation(warm_out[:], warm_in[:], ACT.Gelu_apprx_tanh)
        nc.vector.memset(w_scales[:].bitcast(I32), 0)
        nc.scalar.dma_start(w_words[:].bitcast(I32), w1_words[0].bitcast(I32))
        for q in range(4):
            nc.scalar.dma_start(
                w_scales[32 * q : 32 * q + 4, :].bitcast(I32),
                w1_scales[0, 4 * q : 4 * q + 4, :].bitcast(I32),
            )

        rows = xT.rearrange("(p j) c -> p j c", j=PACK)
        nc.sync.dma_start(first_two[:], rows[:, 0:2, :].rearrange("p j c -> p (j c)"))
        nc.sync.dma_start(offs_t[:], offs)
        nc.sync.dma_start(planes[2], rows[:, 2, :])
        nc.sync.dma_start(planes[3], rows[:, 3, :])
        nc.sync.dma_start(frac_t[:], frac)
        nc.sync.dma_start(right_t[:], right)
        nc.sync.dma_start(left_t[:], left)

        def entries(a, b):
            return offs_t[:, a // 16 : b // 16]

        def fetch(t, a, b, tag):
            whole_tile_form = t >= 2 and b - a >= PIECE
            loose = keep.tile([P, b - a], BF16 if whole_tile_form else F32, name="loose", tag=tag, align_bytes=64)
            nc.scalar.activation(loose[:], planes[t].indirect(entries(a, b)), ACT.Copy)
            return loose

        last = PACK - 1
        for t in range(PACK):
            mine = POOL_FROM if t < 2 else HALF
            nc.vector.tensor_copy(grouped[:, :mine, t], planes[t].indirect(entries(0, mine)))
            if t < 2:
                nc.gpsimd.tensor_copy(grouped[:, POOL_FROM:, t], fetch(t, POOL_FROM, S, "for_pool%d" % t)[:])
                continue
            nc.gpsimd.tensor_copy(grouped[:, POOL_FIRST:, t], fetch(t, POOL_FIRST, S, "first%d" % t)[:])
            nc.gpsimd.tensor_copy(grouped[:, POOL_FROM:POOL_FIRST, t], fetch(t, POOL_FROM, POOL_FIRST, "second%d" % t)[:])
            head = fetch(t, HALF, SCALAR_CUT, "head%d" % t)
            tail = fetch(t, SCALAR_CUT, POOL_FROM, "tail%d" % t)
            if t < last:
                nc.vector.tensor_copy(grouped[:, HALF:VECTOR_TO, t], head[:, : VECTOR_TO - HALF])
            nc.scalar.copy(grouped[:, VECTOR_TO:SCALAR_CUT, t], head[:, VECTOR_TO - HALF :])
            nc.scalar.copy(grouped[:, SCALAR_CUT:POOL_FROM, t], tail[:])

        all_codes = keep.tile([P, S], U32, name="all_codes", tag="second%d" % last, align_bytes=64)
        scales = keep.tile([P, S], U8, name="scales", align_bytes=64)

        def codes(a, b):
            return all_codes[:, a:b].bitcast(FP8X4)

        def quantise(a, b):
            nc.vector.quantize_mx(out=codes(a, b), scales=scales[:, a:b], in_=grouped[:, a:b, :].rearrange("p c t -> p (c t)"))

        def project(i):
            a, b = i * PIECE, (i + 1) * PIECE
            acc = psum.tile([P, PIECE], F32, name="acc%d" % i)
            nc.tensor.matmul_mx(
                out=acc[:],
                lhsT=w_words[:].bitcast(FP4X4),
                lhsT_scale=w_scales[:],
                rhs=codes(a, b),
                rhs_scale=scales[:, a:b],
                start=True,
                stop=True,
            )
            nc.scalar.activation(y[:, a:b], acc[:], ACT.Gelu_apprx_tanh)

        quantise(7 * PIECE, S)
        project(7)
        nc.vector.tensor_copy(grouped[:, HALF:VECTOR_TO, last], head[:, : VECTOR_TO - HALF])
        for i in range(7):
            quantise(i * PIECE, (i + 1) * PIECE)
            project(i)

        rest_t = grouped[:, 5 * PIECE : 7 * PIECE, :].rearrange("p c t -> p (c t)").bitcast(F32)
        nc.vector.tensor_scalar(rest_t, frac_t[:], -1.0, 1.0, ALU.mult, ALU.add)

        picked = keep.tile([P, V], F32, name="picked")
        lo = keep.tile([P, V], F32, name="lo")
        hi = keep.tile([P, V], F32, name="hi")
        res = keep.tile([P, V], F32, name="res")

        parts = (slice(0, LEFT_FIRST), slice(LEFT_FIRST, V))
        for cols in parts:
            nc.scalar.activation(picked[:, cols], y[:].indirect(left_t[:, cols.start // 16 : cols.stop // 16]), ACT.Copy)
        nc.vector.tensor_tensor(hi[:], y[:].indirect(right_t[:]), frac_t[:], ALU.mult)
        for cols in parts:
            nc.vector.tensor_tensor(lo[:, cols], picked[:, cols], rest_t[:, cols], ALU.mult)
        for cols, queue in zip((slice(0, STORE_FIRST), slice(STORE_FIRST, V)), (nc.scalar, nc.sync)):
            nc.vector.tensor_tensor(res[:, cols], lo[:, cols], hi[:, cols], ALU.add)
            queue.dma_start(out[:, cols], res[:, cols])
